import numpy as np
import ml_dtypes


def mxq(x, axis, fmt="e4m3"):
    dtype, down = {"e4m3": (ml_dtypes.float8_e4m3fn, 7), "e5m2": (ml_dtypes.float8_e5m2, 14)}[fmt]
    v = np.moveaxis(np.asarray(x, np.float32).astype(ml_dtypes.bfloat16).astype(np.float64), axis, -1)
    blocks = v.reshape(v.shape[:-1] + (-1, 32))
    amax = np.abs(blocks).max(-1, keepdims=True)
    byte = np.maximum(np.where(amax > 0, np.frexp(amax)[1] - 1 + 127, 0) - down, 1)
    scale = np.exp2(byte - 127.0)
    codes = (blocks / scale).astype(np.float32).astype(dtype).astype(np.float64)
    return np.moveaxis((codes * scale).reshape(v.shape), -1, axis)


WIDE = False


def mx_kscale(k):
    if not WIDE:
        return np.ones(k)
    levels = np.array([10, -10, 5, -5, 0])
    if k % 512:
        return np.exp2(np.random.permutation(np.resize(levels, k // 32))).repeat(32)
    a = np.empty((k // 512, 16))
    for p in range(k // 512):
        a[p, :8] = np.random.permutation(np.resize(levels, 8))
        for g in range(8):
            far = levels[np.abs(levels - a[p, g]) >= 10]
            a[p, g + 8] = far[np.random.randint(len(far))]
    return np.exp2(a.ravel()).repeat(32)


def f64(x):
    return np.asarray(x).astype(np.float64)


def striped(idx):
    return np.tile(idx.reshape(-1, 16).T, (8, 1)).astype(np.uint16)


def unstriped(offs):
    return offs[:16].T.reshape(-1).astype(np.int64)


E2M1 = np.array([0.0, 0.5, 1.0, 1.5, 2.0, 3.0, 4.0, 6.0, -0.0, -0.5, -1.0, -1.5, -2.0, -3.0, -4.0, -6.0])


def pack_weight(w, fmt):
    k, n = w.shape
    w = f64(np.asarray(w, np.float32).astype(ml_dtypes.bfloat16)).reshape(k // 32, 32, n)
    amax = np.abs(w).max(1)
    if fmt == "e4m3":
        byte = np.frexp(amax)[1] - 1 + 127 - 7
    else:
        mant, ex = np.frexp(amax / 6.0)
        byte = np.where(mant > 0.5, ex, ex - 1) + 127
    byte = np.clip(np.where(amax > 0, byte, 1), 1, 254)
    scaled = (w * np.exp2(127.0 - byte)[:, None, :]).reshape(k, n).astype(np.float32)
    by_word = np.ascontiguousarray(scaled.reshape(k // 512, 128, 4, n).transpose(0, 1, 3, 2))
    if fmt == "e4m3":
        words = by_word.astype(ml_dtypes.float8_e4m3fn).view(np.uint8)
    else:
        c = by_word.astype(ml_dtypes.float4_e2m1fn).view(np.uint8) & 0xF
        words = (c[..., 0::2] | (c[..., 1::2] << 4)).reshape(k // 512, 128, 2 * n)
    return np.ascontiguousarray(words), np.ascontiguousarray(byte.astype(np.uint8).reshape(k // 512, 16, n))


def unpack_weight(words, scales, fmt):
    g, _, n = scales.shape
    words = np.ascontiguousarray(words).reshape(g, 128, n, -1)
    if fmt == "e4m3":
        vals = words.view(ml_dtypes.float8_e4m3fn).astype(np.float64)
    else:
        nib = np.empty((g, 128, n, 4), np.uint8)
        nib[..., 0::2] = words & 0xF
        nib[..., 1::2] = words >> 4
        vals = E2M1[nib]
    vals = vals * np.repeat(np.exp2(scales.astype(np.float64) - 127.0), 8, axis=1)[..., None]
    return vals.transpose(0, 1, 3, 2).reshape(g * 512, n)


def gelu(v):
    return 0.5 * v * (1.0 + np.tanh(np.sqrt(2.0 / np.pi) * (v + 0.044715 * v**3)))


K, T, E, C, H, N = 512, 1280, 6, 128, 512, 128


def by_expert(wq, xq):
    return np.concatenate([wq[e].T @ xq[:, e * C:(e + 1) * C] for e in range(E)], axis=1)


def setup_inputs():
    n = np.random.standard_normal
    s = mx_kscale(K)[:, None]
    u = mx_kscale(H)
    x = pack_weight(n((K, T)) * s, "e4m3")
    return {
        "x_words": x[0],
        "x_scales": x[1],
        "xr": n((N, T)).astype(np.float32),
        "w1": (n((E, K, H)) / np.sqrt(K) / s[None]).astype(np.float32),
        "w3": (n((E, K, H)) / np.sqrt(K) / s[None] * u[None, None, :]).astype(np.float32),
        "w2": (n((E, H, N)) / np.sqrt(H) / u[None, :, None]).astype(np.float32),
        "gate": np.tile(np.random.uniform(0.2, 1.0, E * C), (N, 1)).astype(np.float32),
        "offs": striped(np.random.permutation(T)[:E * C]),
    }


def reference(x_words, x_scales, xr, w1, w3, w2, gate, offs):
    idx = unstriped(offs)
    xq = unpack_weight(x_words, x_scales, "e4m3")[:, idx]
    h = gelu(by_expert(mxq(f64(w1), 1, "e4m3"), xq))
    h = h * by_expert(mxq(f64(w3), 1, "e4m3"), xq)
    y = by_expert(mxq(f64(w2), 1, "e4m3"), mxq(h, 0, "e4m3"))
    out = f64(xr).copy()
    out[:, idx] += f64(gate) * y
    return out

@@ -1,0 +1,142 @@
+from contextlib import ExitStack
+
+import concourse.mybir as mybir
+
+K, T, E, C, H, N = 512, 1280, 6, 128, 512, 128
+S = E * C
+FLOPS = 2 * S * (2 * K * H + H * N)
+
+F32 = mybir.dt.float32
+BF16 = mybir.dt.bfloat16
+I32 = mybir.dt.int32
+U32 = mybir.dt.uint32
+U16 = mybir.dt.uint16
+U8 = mybir.dt.uint8
+FP8X4 = mybir.dt.float8_e4m3fn_x4
+MULT = mybir.AluOpType.mult
+ADD = mybir.AluOpType.add
+GELU = mybir.ActivationFunctionType.Gelu_apprx_tanh
+
+P = 128
+PACK = 4
+PER_COL = 16
+SCALAR_SHARE = 104
+SCALAR_SHARE_LAST = 44
+GATHER_CUTS = (0, 256, 768)
+SCATTER_CUTS = (0, 256, 448, 608, 768)
+STORE_CUTS = (0, 512, 1024, 1280)
+
+
+def tile_moe_res_glu_gelu_kernel(tc, x_words, x_scales, xr, w1, w3, w2, gate, offs, out):
+    nc = tc.nc
+    with ExitStack() as ctx:
+        keep = ctx.enter_context(tc.tile_pool(name="keep", bufs=1))
+        ring = ctx.enter_context(tc.tile_pool(name="ring", bufs=3))
+        psum = ctx.enter_context(tc.psum_pool(name="psum", bufs=2))
+
+        offsets = keep.tile([P, S // PER_COL], U16, name="offsets")
+        tok_words = keep.tile([P, T], U32, name="tok_words")
+        tok_scales = keep.tile([P, T], U8, name="tok_scales")
+        slot_words = keep.tile([P, S], U32, name="slot_words", align_bytes=64)
+        slot_scales = keep.tile([P, S], U8, name="slot_scales", align_bytes=64)
+        window = keep.tile([P, T], F32, name="window")
+        y_slots = keep.tile([P, S], F32, name="y_slots")
+        gate_sb = keep.tile([P, S], F32, name="gate_sb")
+        xr_sb = keep.tile([P, T], F32, name="xr_sb")
+
+        nc.vector.memset(tok_scales[:].bitcast(I32), 0)
+        nc.vector.memset(window[:], 0.0)
+
+        nc.sync.dma_start(offsets[:], offs)
+        nc.sync.dma_start(tok_words[:].bitcast(I32), x_words[0].rearrange("p t r -> p (t r)").bitcast(I32))
+        scale_rows = x_scales[0].bitcast(I32)
+        for r in range(4):
+            nc.sync.dma_start(tok_scales[r:P:32, :].bitcast(I32), scale_rows[r:16:4, :])
+
+        raw = {}
+        for e in range(E):
+            for name, w, width in (("w1", w1, H), ("w3", w3, H), ("w2", w2, N)):
+                raw[name, e] = keep.tile([P, PACK, width], F32, name=f"{name}_raw{e}")
+                nc.sync.dma_start(raw[name, e][:], w[e].rearrange("(p j) c -> p j c", j=PACK))
+            if e == 1:
+                nc.sync.dma_start(gate_sb[:], gate)
+        nc.sync.dma_start(xr_sb[:], xr)
+
+        for a, b in zip(GATHER_CUTS, GATHER_CUTS[1:]):
+            piece = offsets[:, a // PER_COL : b // PER_COL]
+            nc.vector.tensor_copy(slot_words[:, a:b], tok_words[:].indirect(piece))
+            nc.vector.tensor_copy(slot_scales[:, a:b], tok_scales[:].indirect(piece))
+
+        def quantize(grouped, tag):
+            width = grouped.shape[1] // PACK
+            codes = ring.tile([P, width], U32, name=tag + "_codes", align_bytes=64)
+            scales = ring.tile([P, width], U8, name=tag + "_scales", align_bytes=64)
+            nc.vector.quantize_mx(out=codes[:].bitcast(FP8X4), scales=scales[:], in_=grouped[:])
+            return codes, scales
+
+        def first_layer_sums(name, e):
+            share = SCALAR_SHARE_LAST if (name, e) == ("w3", E - 1) else SCALAR_SHARE
+            grouped = ring.tile([P, PACK * H], BF16, name=name + "_grouped", align_bytes=64)
+            dst = grouped[:].rearrange("p (t m j) -> p m j t", t=PACK, j=PACK)
+            src = raw[name, e][:].rearrange("p j (m t) -> p m j t", t=PACK)
+            nc.scalar.copy(dst[:, :share], src[:, :share])
+            nc.vector.tensor_copy(dst[:, share:], src[:, share:])
+            codes, scales = quantize(grouped, name)
+            sums = psum.tile([P, PACK, C], F32, name=name + "_sums")
+            slots = slice(e * C, (e + 1) * C)
+            for t in range(PACK):
+                cols = slice(t * P, (t + 1) * P)
+                nc.tensor.matmul_mx(
+                    out=sums[:, t, :],
+                    lhsT=codes[:, cols].bitcast(FP8X4),
+                    lhsT_scale=scales[:, cols],
+                    rhs=slot_words[:, slots].bitcast(FP8X4),
+                    rhs_scale=slot_scales[:, slots],
+                    start=True,
+                    stop=True,
+                )
+            return sums[:].rearrange("p t c -> p c t")
+
+        def hidden(e):
+            a = first_layer_sums("w1", e)
+            act = ring.tile([P, C, PACK], F32, name="act")
+            nc.scalar.activation(act[:], a, GELU)
+            b = first_layer_sums("w3", e)
+            h = ring.tile([P, C * PACK], BF16, name="h", align_bytes=64)
+            nc.vector.tensor_tensor(h[:].rearrange("p (c t) -> p c t", t=PACK), b, act[:], MULT)
+            return h
+
+        def second_layer(e, h):
+            grouped = ring.tile([P, PACK * N], BF16, name="w2_grouped", align_bytes=64)
+            dst = grouped[:].rearrange("p (c i j) -> p c j i", i=4, j=PACK)
+            src = raw["w2", e][:].rearrange("p j (c i) -> p c j i", i=4)
+            if e == E - 1:
+                nc.scalar.copy(dst, src)
+            else:
+                nc.vector.tensor_copy(dst, src)
+            w_codes, w_scales = quantize(grouped, "w2")
+            h_codes, h_scales = quantize(h, "h")
+            y = psum.tile([P, C], F32, name="y")
+            nc.tensor.matmul_mx(
+                out=y[:],
+                lhsT=w_codes[:].bitcast(FP8X4),
+                lhsT_scale=w_scales[:],
+                rhs=h_codes[:].bitcast(FP8X4),
+                rhs_scale=h_scales[:],
+                start=True,
+                stop=True,
+            )
+            nc.scalar.copy(y_slots[:, e * C : (e + 1) * C], y[:])
+            for a, b in zip(SCATTER_CUTS, SCATTER_CUTS[1:]):
+                if e * C < b <= (e + 1) * C:
+                    piece = offsets[:, a // PER_COL : b // PER_COL]
+                    nc.vector.tensor_tensor(window[:].indirect(piece), y_slots[:, a:b], gate_sb[:, a:b], MULT)
+
+        for e in range(E):
+            second_layer(e, hidden(e))
+
+        for i, (a, b) in enumerate(zip(STORE_CUTS, STORE_CUTS[1:])):
+            result = keep.tile([P, b - a], F32, name=f"result{i}")
+            nc.vector.tensor_tensor(result[:], window[:, a:b], xr_sb[:, a:b], ADD)
+            queue = nc.sync if i % 2 == 0 else nc.scalar
+            queue.dma_start(out[:, a:b], result[:])

@@ -20,10 +20,7 @@ GELU = mybir.ActivationFunctionType.Gelu_apprx_tanh
 P = 128
 PACK = 4
 PER_COL = 16
-SCALAR_SHARE = 104
-SCALAR_SHARE_LAST = 44
 GATHER_CUTS = (0, 256, 768)
-SCATTER_CUTS = (0, 256, 448, 608, 768)
 STORE_CUTS = (0, 512, 1024, 1280)
 
 
@@ -31,7 +28,7 @@ def tile_moe_res_glu_gelu_kernel(tc, x_words, x_scales, xr, w1, w3, w2, gate, of
     nc = tc.nc
     with ExitStack() as ctx:
         keep = ctx.enter_context(tc.tile_pool(name="keep", bufs=1))
-        ring = ctx.enter_context(tc.tile_pool(name="ring", bufs=3))
+        ring = ctx.enter_context(tc.tile_pool(name="ring", bufs=2))
         psum = ctx.enter_context(tc.psum_pool(name="psum", bufs=2))
 
         offsets = keep.tile([P, S // PER_COL], U16, name="offsets")
@@ -40,12 +37,13 @@ def tile_moe_res_glu_gelu_kernel(tc, x_words, x_scales, xr, w1, w3, w2, gate, of
         slot_words = keep.tile([P, S], U32, name="slot_words", align_bytes=64)
         slot_scales = keep.tile([P, S], U8, name="slot_scales", align_bytes=64)
         window = keep.tile([P, T], F32, name="window")
-        y_slots = keep.tile([P, S], F32, name="y_slots")
         gate_sb = keep.tile([P, S], F32, name="gate_sb")
         xr_sb = keep.tile([P, T], F32, name="xr_sb")
+        zeros = keep.tile([P, C], F32, name="zeros")
 
         nc.vector.memset(tok_scales[:].bitcast(I32), 0)
-        nc.vector.memset(window[:], 0.0)
+        nc.vector.memset(zeros[:], 0.0)
+        nc.scalar.activation(window[:], zeros[:, 0:1].to_broadcast([P, T]), GELU)
 
         nc.sync.dma_start(offsets[:], offs)
         nc.sync.dma_start(tok_words[:].bitcast(I32), x_words[0].rearrange("p t r -> p (t r)").bitcast(I32))
@@ -58,7 +56,7 @@ def tile_moe_res_glu_gelu_kernel(tc, x_words, x_scales, xr, w1, w3, w2, gate, of
             for name, w, width in (("w1", w1, H), ("w3", w3, H), ("w2", w2, N)):
                 raw[name, e] = keep.tile([P, PACK, width], F32, name=f"{name}_raw{e}")
                 nc.sync.dma_start(raw[name, e][:], w[e].rearrange("(p j) c -> p j c", j=PACK))
-            if e == 1:
+            if e == 0:
                 nc.sync.dma_start(gate_sb[:], gate)
         nc.sync.dma_start(xr_sb[:], xr)
 
@@ -71,21 +69,19 @@ def tile_moe_res_glu_gelu_kernel(tc, x_words, x_scales, xr, w1, w3, w2, gate, of
             width = grouped.shape[1] // PACK
             codes = ring.tile([P, width], U32, name=tag + "_codes", align_bytes=64)
             scales = ring.tile([P, width], U8, name=tag + "_scales", align_bytes=64)
-            nc.vector.quantize_mx(out=codes[:].bitcast(FP8X4), scales=scales[:], in_=grouped[:])
+            nc.vector.quantize_mx(out=codes[:].bitcast(FP8X4), scales=scales[:], in_=grouped)
             return codes, scales
 
-        def first_layer_sums(name, e):
-            share = SCALAR_SHARE_LAST if (name, e) == ("w3", E - 1) else SCALAR_SHARE
-            grouped = ring.tile([P, PACK * H], BF16, name=name + "_grouped", align_bytes=64)
-            dst = grouped[:].rearrange("p (t m j) -> p m j t", t=PACK, j=PACK)
-            src = raw[name, e][:].rearrange("p j (m t) -> p m j t", t=PACK)
-            nc.scalar.copy(dst[:, :share], src[:, :share])
-            nc.vector.tensor_copy(dst[:, share:], src[:, share:])
-            codes, scales = quantize(grouped, name)
-            sums = psum.tile([P, PACK, C], F32, name=name + "_sums")
+        def regroup(copy, grouped, name, e, t0, t1):
+            dst = grouped.rearrange("p (t m j) -> p m j t", t=t1 - t0, j=PACK)
+            src = raw[name, e][:].rearrange("p j (m t) -> p t m j", t=PACK)[:, t0:t1].rearrange("p t m j -> p m j t")
+            copy(dst, src)
+
+        def multiply(sums, operand, e, t0, t1):
+            codes, scales = operand
             slots = slice(e * C, (e + 1) * C)
-            for t in range(PACK):
-                cols = slice(t * P, (t + 1) * P)
+            for t in range(t0, t1):
+                cols = slice((t - t0) * P, (t - t0 + 1) * P)
                 nc.tensor.matmul_mx(
                     out=sums[:, t, :],
                     lhsT=codes[:, cols].bitcast(FP8X4),
@@ -95,27 +91,46 @@ def tile_moe_res_glu_gelu_kernel(tc, x_words, x_scales, xr, w1, w3, w2, gate, of
                     start=True,
                     stop=True,
                 )
-            return sums[:].rearrange("p t c -> p c t")
 
-        def hidden(e):
-            a = first_layer_sums("w1", e)
+        def gate_results(e, y, gated):
+            nc.vector.tensor_tensor(gated, y[:], gate_sb[:, e * C : (e + 1) * C], MULT)
+
+        def scatter_results(e, gated):
+            piece = offsets[:, e * C // PER_COL : (e + 1) * C // PER_COL]
+            nc.vector.tensor_tensor(window[:].indirect(piece), gated, zeros[:], ADD)
+
+        y = None
+        for e in range(E):
+            a = psum.tile([P, PACK, C], F32, name="a")
+            b = psum.tile([P, PACK, C], F32, name="b")
+            w1_grouped = ring.tile([P, PACK * H], BF16, name="w1_grouped", align_bytes=64)
+            w3_low = ring.tile([P, 1024], BF16, name="w3_low", align_bytes=64)
+            w3_high = ring.tile([P, 1024], BF16, name="w3_high", align_bytes=64)
+            regroup(nc.scalar.copy, w1_grouped[:], "w1", e, 0, 4)
+            regroup(nc.scalar.copy, w3_low[:], "w3", e, 0, 2)
+            multiply(a, quantize(w1_grouped[:], "w1"), e, 0, 4)
+            regroup(nc.vector.tensor_copy, w3_high[:], "w3", e, 2, 4)
             act = ring.tile([P, C, PACK], F32, name="act")
-            nc.scalar.activation(act[:], a, GELU)
-            b = first_layer_sums("w3", e)
-            h = ring.tile([P, C * PACK], BF16, name="h", align_bytes=64)
-            nc.vector.tensor_tensor(h[:].rearrange("p (c t) -> p c t", t=PACK), b, act[:], MULT)
-            return h
+            nc.scalar.activation(act[:], a[:].rearrange("p t c -> p c t"), GELU)
+            multiply(b, quantize(w3_high[:], "w3_high"), e, 2, 4)
+            if e > 0:
+                gated = w3_high[:, : 2 * C].bitcast(F32)
+                gate_results(e - 1, y, gated)
+            multiply(b, quantize(w3_low[:], "w3_low"), e, 0, 2)
 
-        def second_layer(e, h):
-            grouped = ring.tile([P, PACK * N], BF16, name="w2_grouped", align_bytes=64)
-            dst = grouped[:].rearrange("p (c i j) -> p c j i", i=4, j=PACK)
+            w2_grouped = ring.tile([P, PACK * N], BF16, name="w2_grouped", align_bytes=64)
+            dst = w2_grouped[:].rearrange("p (c i j) -> p c j i", i=4, j=PACK)
             src = raw["w2", e][:].rearrange("p j (c i) -> p c j i", i=4)
             if e == E - 1:
                 nc.scalar.copy(dst, src)
             else:
                 nc.vector.tensor_copy(dst, src)
-            w_codes, w_scales = quantize(grouped, "w2")
-            h_codes, h_scales = quantize(h, "h")
+            if e > 0:
+                scatter_results(e - 1, gated)
+            h = ring.tile([P, C * PACK], BF16, name="h", align_bytes=64)
+            nc.vector.tensor_tensor(h[:].rearrange("p (c t) -> p c t", t=PACK), b[:].rearrange("p t c -> p c t"), act[:], MULT)
+            w_codes, w_scales = quantize(w2_grouped[:], "w2")
+            h_codes, h_scales = quantize(h[:], "h")
             y = psum.tile([P, C], F32, name="y")
             nc.tensor.matmul_mx(
                 out=y[:],
@@ -126,17 +141,12 @@ def tile_moe_res_glu_gelu_kernel(tc, x_words, x_scales, xr, w1, w3, w2, gate, of
                 start=True,
                 stop=True,
             )
-            nc.scalar.copy(y_slots[:, e * C : (e + 1) * C], y[:])
-            for a, b in zip(SCATTER_CUTS, SCATTER_CUTS[1:]):
-                if e * C < b <= (e + 1) * C:
-                    piece = offsets[:, a // PER_COL : b // PER_COL]
-                    nc.vector.tensor_tensor(window[:].indirect(piece), y_slots[:, a:b], gate_sb[:, a:b], MULT)
+        last_gated = keep.tile([P, C], F32, name="last_gated")
+        gate_results(E - 1, y, last_gated[:])
+        scatter_results(E - 1, last_gated[:])
 
-        for e in range(E):
-            second_layer(e, hidden(e))
-
-        for i, (a, b) in enumerate(zip(STORE_CUTS, STORE_CUTS[1:])):
-            result = keep.tile([P, b - a], F32, name=f"result{i}")
-            nc.vector.tensor_tensor(result[:], window[:, a:b], xr_sb[:, a:b], ADD)
+        for i, (lo, hi) in enumerate(zip(STORE_CUTS, STORE_CUTS[1:])):
+            result = keep.tile([P, hi - lo], F32, name=f"result{i}")
+            nc.vector.tensor_tensor(result[:], window[:, lo:hi], xr_sb[:, lo:hi], ADD)
             queue = nc.sync if i % 2 == 0 else nc.scalar
-            queue.dma_start(out[:, a:b], result[:])
+            queue.dma_start(out[:, lo:hi], result[:])

@@ -1,6 +1,7 @@
 from contextlib import ExitStack
 
 import concourse.mybir as mybir
+from concourse.masks import make_identity
 
 K, T, E, C, H, N = 512, 1280, 6, 128, 512, 128
 S = E * C
@@ -19,9 +20,11 @@ GELU = mybir.ActivationFunctionType.Gelu_apprx_tanh
 
 P = 128
 PACK = 4
+PAIR = 2
 PER_COL = 16
 GATHER_CUTS = (0, 256, 768)
-STORE_CUTS = (0, 512, 1024, 1280)
+STORE_CUTS = (0, 256, 640, 1024, 1280)
+W2_ON_SCALAR_FROM = 4
 
 
 def tile_moe_res_glu_gelu_kernel(tc, x_words, x_scales, xr, w1, w3, w2, gate, offs, out):
@@ -37,12 +40,16 @@ def tile_moe_res_glu_gelu_kernel(tc, x_words, x_scales, xr, w1, w3, w2, gate, of
         slot_words = keep.tile([P, S], U32, name="slot_words", align_bytes=64)
         slot_scales = keep.tile([P, S], U8, name="slot_scales", align_bytes=64)
         window = keep.tile([P, T], F32, name="window")
-        gate_sb = keep.tile([P, S], F32, name="gate_sb")
+        gate_rows = keep.tile([P, C], F32, name="gate_rows")
+        gate_cols = keep.tile([P, E], F32, name="gate_cols")
+        gate_sb = keep.tile([P, E, C], F32, name="gate_sb")
         xr_sb = keep.tile([P, T], F32, name="xr_sb")
         zeros = keep.tile([P, C], F32, name="zeros")
+        identity = keep.tile([P, P], F32, name="identity")
 
         nc.vector.memset(tok_scales[:].bitcast(I32), 0)
         nc.vector.memset(zeros[:], 0.0)
+        make_identity(nc, identity[:])
         nc.scalar.activation(window[:], zeros[:, 0:1].to_broadcast([P, T]), GELU)
 
         nc.sync.dma_start(offsets[:], offs)
@@ -50,40 +57,58 @@ def tile_moe_res_glu_gelu_kernel(tc, x_words, x_scales, xr, w1, w3, w2, gate, of
         scale_rows = x_scales[0].bitcast(I32)
         for r in range(4):
             nc.sync.dma_start(tok_scales[r:P:32, :].bitcast(I32), scale_rows[r:16:4, :])
+        nc.sync.dma_start(gate_rows[:], gate.rearrange("n (e c) -> (n e) c", c=C)[0:P, :])
 
         raw = {}
+
+        def load(name, w, e):
+            raw[name, e] = keep.tile([P, PACK, w.shape[2]], F32, name=f"{name}_raw{e}")
+            nc.sync.dma_start(raw[name, e][:], w[e].rearrange("(p j) c -> p j c", j=PACK))
+
         for e in range(E):
-            for name, w, width in (("w1", w1, H), ("w3", w3, H), ("w2", w2, N)):
-                raw[name, e] = keep.tile([P, PACK, width], F32, name=f"{name}_raw{e}")
-                nc.sync.dma_start(raw[name, e][:], w[e].rearrange("(p j) c -> p j c", j=PACK))
-            if e == 0:
-                nc.sync.dma_start(gate_sb[:], gate)
+            load("w1", w1, e)
+            load("w3", w3, e)
+            if e < E - 2:
+                load("w2", w2, e)
+        load("w2", w2, E - 2)
+        load("w2", w2, E - 1)
         nc.sync.dma_start(xr_sb[:], xr)
 
-        for a, b in zip(GATHER_CUTS, GATHER_CUTS[1:]):
-            piece = offsets[:, a // PER_COL : b // PER_COL]
-            nc.vector.tensor_copy(slot_words[:, a:b], tok_words[:].indirect(piece))
-            nc.vector.tensor_copy(slot_scales[:, a:b], tok_scales[:].indirect(piece))
+        turned = psum.tile([P, C], F32, name="y")
+        nc.tensor.transpose(turned[:], gate_rows[:], identity[:])
+        nc.scalar.copy(gate_cols[:], turned[:, :E])
+        for tag, e0, e1 in (("a", 0, PACK), ("b", PACK, E)):
+            spread = psum.tile([P, PACK, C], F32, name=tag)
+            for e in range(e0, e1):
+                nc.tensor.transpose(spread[:, e - e0, :], gate_cols[:, e : e + 1].to_broadcast([P, P]), identity[:])
+            nc.scalar.copy(gate_sb[:, e0:e1, :], spread[:, : e1 - e0, :])
+
+        for lo, hi in zip(GATHER_CUTS, GATHER_CUTS[1:]):
+            piece = offsets[:, lo // PER_COL : hi // PER_COL]
+            nc.vector.tensor_copy(slot_words[:, lo:hi], tok_words[:].indirect(piece))
+            nc.vector.tensor_copy(slot_scales[:, lo:hi], tok_scales[:].indirect(piece))
 
         def quantize(grouped, tag):
             width = grouped.shape[1] // PACK
             codes = ring.tile([P, width], U32, name=tag + "_codes", align_bytes=64)
             scales = ring.tile([P, width], U8, name=tag + "_scales", align_bytes=64)
-            nc.vector.quantize_mx(out=codes[:].bitcast(FP8X4), scales=scales[:], in_=grouped)
+            nc.vector.quantize_mx(out=codes[:].bitcast(FP8X4), scales=scales[:], in_=grouped[:])
             return codes, scales
 
-        def regroup(copy, grouped, name, e, t0, t1):
-            dst = grouped.rearrange("p (t m j) -> p m j t", t=t1 - t0, j=PACK)
-            src = raw[name, e][:].rearrange("p j (m t) -> p t m j", t=PACK)[:, t0:t1].rearrange("p t m j -> p m j t")
+        def regroup(copy, name, e, half):
+            grouped = ring.tile([P, PAIR * P * PACK], BF16, name=f"{name}_grouped{half}", align_bytes=64)
+            dst = grouped[:].rearrange("p (t m j) -> p m j t", t=PAIR, j=PACK)
+            src = raw[name, e][:].rearrange("p j (m u t) -> p u m j t", u=PACK // PAIR, t=PAIR)[:, half]
             copy(dst, src)
+            return grouped
 
-        def multiply(sums, operand, e, t0, t1):
-            codes, scales = operand
+        def multiply(sums, grouped, name, e, half):
+            codes, scales = quantize(grouped, f"{name}_{half}")
             slots = slice(e * C, (e + 1) * C)
-            for t in range(t0, t1):
-                cols = slice((t - t0) * P, (t - t0 + 1) * P)
+            for t in range(PAIR):
+                cols = slice(t * P, (t + 1) * P)
                 nc.tensor.matmul_mx(
-                    out=sums[:, t, :],
+                    out=sums[:, half * PAIR + t, :],
                     lhsT=codes[:, cols].bitcast(FP8X4),
                     lhsT_scale=scales[:, cols],
                     rhs=slot_words[:, slots].bitcast(FP8X4),
@@ -92,55 +117,76 @@ def tile_moe_res_glu_gelu_kernel(tc, x_words, x_scales, xr, w1, w3, w2, gate, of
                     stop=True,
                 )
 
+        def regroup_w2(e):
+            grouped = ring.tile([P, PACK * N], BF16, name="w2_grouped", align_bytes=64)
+            dst = grouped[:].rearrange("p (c i j) -> p c j i", i=4, j=PACK)
+            src = raw["w2", e][:].rearrange("p j (c i) -> p c j i", i=4)
+            copy = nc.scalar.copy if e >= W2_ON_SCALAR_FROM else nc.vector.tensor_copy
+            copy(dst, src)
+            return grouped
+
+        def second_product(w_operand, h_operand):
+            y = psum.tile([P, C], F32, name="y")
+            nc.tensor.matmul_mx(
+                out=y[:],
+                lhsT=w_operand[0][:].bitcast(FP8X4),
+                lhsT_scale=w_operand[1][:],
+                rhs=h_operand[0][:].bitcast(FP8X4),
+                rhs_scale=h_operand[1][:],
+                start=True,
+                stop=True,
+            )
+            return y
+
         def gate_results(e, y, gated):
-            nc.vector.tensor_tensor(gated, y[:], gate_sb[:, e * C : (e + 1) * C], MULT)
+            nc.vector.tensor_tensor(gated, y[:], gate_sb[:, e, :], MULT)
 
         def scatter_results(e, gated):
             piece = offsets[:, e * C // PER_COL : (e + 1) * C // PER_COL]
             nc.vector.tensor_tensor(window[:].indirect(piece), gated, zeros[:], ADD)
 
-        y = None
+        y = h_operand = None
         for e in range(E):
+            last = e == E - 1
             a = psum.tile([P, PACK, C], F32, name="a")
             b = psum.tile([P, PACK, C], F32, name="b")
-            w1_grouped = ring.tile([P, PACK * H], BF16, name="w1_grouped", align_bytes=64)
-            w3_low = ring.tile([P, 1024], BF16, name="w3_low", align_bytes=64)
-            w3_high = ring.tile([P, 1024], BF16, name="w3_high", align_bytes=64)
-            regroup(nc.scalar.copy, w1_grouped[:], "w1", e, 0, 4)
-            regroup(nc.scalar.copy, w3_low[:], "w3", e, 0, 2)
-            multiply(a, quantize(w1_grouped[:], "w1"), e, 0, 4)
-            regroup(nc.vector.tensor_copy, w3_high[:], "w3", e, 2, 4)
-            act = ring.tile([P, C, PACK], F32, name="act")
-            nc.scalar.activation(act[:], a[:].rearrange("p t c -> p c t"), GELU)
-            multiply(b, quantize(w3_high[:], "w3_high"), e, 2, 4)
-            if e > 0:
+            w1_halves = [regroup(nc.scalar.copy, "w1", e, half) for half in range(2)]
+            w3_low = regroup(nc.scalar.copy, "w3", e, 0)
+            for half in range(2):
+                multiply(a, w1_halves[half], "w1", e, half)
+            w3_high = regroup(nc.vector.tensor_copy, "w3", e, 1)
+            if last:
+                w2_grouped = regroup_w2(e - 1)
+            act = ring.tile([P, C * PACK], F32, name="act")
+            nc.scalar.activation(act[:].rearrange("p (c t) -> p c t", t=PACK), a[:].rearrange("p t c -> p c t"), GELU)
+            multiply(b, w3_high, "w3", e, 1)
+            if 0 < e < E - 1:
                 gated = w3_high[:, : 2 * C].bitcast(F32)
                 gate_results(e - 1, y, gated)
-            multiply(b, quantize(w3_low[:], "w3_low"), e, 0, 2)
-
-            w2_grouped = ring.tile([P, PACK * N], BF16, name="w2_grouped", align_bytes=64)
-            dst = w2_grouped[:].rearrange("p (c i j) -> p c j i", i=4, j=PACK)
-            src = raw["w2", e][:].rearrange("p j (c i) -> p c j i", i=4)
-            if e == E - 1:
-                nc.scalar.copy(dst, src)
-            else:
-                nc.vector.tensor_copy(dst, src)
-            if e > 0:
+            multiply(b, w3_low, "w3", e, 0)
+            if last:
+                y = second_product(quantize(w2_grouped, "w2"), h_operand)
+            if e != E - 2:
+                w2_grouped = regroup_w2(e)
+            if 0 < e < E - 1:
                 scatter_results(e - 1, gated)
             h = ring.tile([P, C * PACK], BF16, name="h", align_bytes=64)
-            nc.vector.tensor_tensor(h[:].rearrange("p (c t) -> p c t", t=PACK), b[:].rearrange("p t c -> p c t"), act[:], MULT)
-            w_codes, w_scales = quantize(w2_grouped[:], "w2")
-            h_codes, h_scales = quantize(h[:], "h")
-            y = psum.tile([P, C], F32, name="y")
-            nc.tensor.matmul_mx(
-                out=y[:],
-                lhsT=w_codes[:].bitcast(FP8X4),
-                lhsT_scale=w_scales[:],
-                rhs=h_codes[:].bitcast(FP8X4),
-                rhs_scale=h_scales[:],
-                start=True,
-                stop=True,
+            nc.vector.tensor_tensor(
+                h[:].rearrange("p (c t) -> p c t", t=PACK),
+                b[:].rearrange("p t c -> p c t"),
+                act[:].rearrange("p (c t) -> p c t", t=PACK),
+                MULT,
             )
+            if last:
+                gated = act[:, :C]
+                gate_results(e - 1, y, gated)
+            if e != E - 2:
+                w2_operand = quantize(w2_grouped, "w2")
+            h_operand = quantize(h, "h")
+            if last:
+                scatter_results(e - 1, gated)
+            if e != E - 2:
+                y = second_product(w2_operand, h_operand)
         last_gated = keep.tile([P, C], F32, name="last_gated")
         gate_results(E - 1, y, last_gated[:])
         scatter_results(E - 1, last_gated[:])

@@ -50,13 +50,13 @@ def tile_moe_res_glu_gelu_kernel(tc, x_words, x_scales, xr, w1, w3, w2, gate, of
         nc.vector.memset(tok_scales[:].bitcast(I32), 0)
         nc.vector.memset(zeros[:], 0.0)
         make_identity(nc, identity[:])
-        nc.scalar.activation(window[:], zeros[:, 0:1].to_broadcast([P, T]), GELU)
 
         nc.sync.dma_start(offsets[:], offs)
         nc.sync.dma_start(tok_words[:].bitcast(I32), x_words[0].rearrange("p t r -> p (t r)").bitcast(I32))
         scale_rows = x_scales[0].bitcast(I32)
         for r in range(4):
-            nc.sync.dma_start(tok_scales[r:P:32, :].bitcast(I32), scale_rows[r:16:4, :])
+            nc.scalar.dma_start(tok_scales[r:P:32, :].bitcast(I32), scale_rows[r:16:4, :])
+        nc.scalar.activation(window[:], zeros[:, 0:1].to_broadcast([P, T]), GELU)
         nc.sync.dma_start(gate_rows[:], gate.rearrange("n (e c) -> (n e) c", c=C)[0:P, :])
 
         raw = {}

@@ -21,20 +21,25 @@ GELU = mybir.ActivationFunctionType.Gelu_apprx_tanh
 P = 128
 PACK = 4
 PAIR = 2
-PER_COL = 16
-GATHER_CUTS = (0, 256, 768)
-STORE_CUTS = (0, 256, 640, 1024, 1280)
-W2_ON_SCALAR_FROM = 4
+RUN = 4
+QUADRANT = 32
+SCALE_ROWS = K // 32
+SLOTS_PER_COL = 16
+RING = 2
+GATHER_CUTS = (0, 2 * C, S)
+STORE_CUTS = (0, 256, 640, 1024, T)
+LATE_W2 = E - 2
+SCALAR_PLACES = 88
 
 
 def tile_moe_res_glu_gelu_kernel(tc, x_words, x_scales, xr, w1, w3, w2, gate, offs, out):
     nc = tc.nc
     with ExitStack() as ctx:
         keep = ctx.enter_context(tc.tile_pool(name="keep", bufs=1))
-        ring = ctx.enter_context(tc.tile_pool(name="ring", bufs=2))
-        psum = ctx.enter_context(tc.psum_pool(name="psum", bufs=2))
+        ring = ctx.enter_context(tc.tile_pool(name="ring", bufs=RING))
+        psum = ctx.enter_context(tc.psum_pool(name="psum", bufs=RING))
 
-        offsets = keep.tile([P, S // PER_COL], U16, name="offsets")
+        offsets = keep.tile([P, S // SLOTS_PER_COL], U16, name="offsets")
         tok_words = keep.tile([P, T], U32, name="tok_words")
         tok_scales = keep.tile([P, T], U8, name="tok_scales")
         slot_words = keep.tile([P, S], U32, name="slot_words", align_bytes=64)
@@ -54,8 +59,9 @@ def tile_moe_res_glu_gelu_kernel(tc, x_words, x_scales, xr, w1, w3, w2, gate, of
         nc.sync.dma_start(offsets[:], offs)
         nc.sync.dma_start(tok_words[:].bitcast(I32), x_words[0].rearrange("p t r -> p (t r)").bitcast(I32))
         scale_rows = x_scales[0].bitcast(I32)
-        for r in range(4):
-            nc.scalar.dma_start(tok_scales[r:P:32, :].bitcast(I32), scale_rows[r:16:4, :])
+        rows_per_quadrant = SCALE_ROWS * QUADRANT // P
+        for r in range(rows_per_quadrant):
+            nc.scalar.dma_start(tok_scales[r:P:QUADRANT, :].bitcast(I32), scale_rows[r:SCALE_ROWS:rows_per_quadrant, :])
         nc.scalar.activation(window[:], zeros[:, 0:1].to_broadcast([P, T]), GELU)
         nc.sync.dma_start(gate_rows[:], gate.rearrange("n (e c) -> (n e) c", c=C)[0:P, :])
 
@@ -68,10 +74,10 @@ def tile_moe_res_glu_gelu_kernel(tc, x_words, x_scales, xr, w1, w3, w2, gate, of
         for e in range(E):
             load("w1", w1, e)
             load("w3", w3, e)
-            if e < E - 2:
+            if e < LATE_W2:
                 load("w2", w2, e)
-        load("w2", w2, E - 2)
-        load("w2", w2, E - 1)
+        for e in range(LATE_W2, E):
+            load("w2", w2, e)
         nc.sync.dma_start(xr_sb[:], xr)
 
         turned = psum.tile([P, C], F32, name="y")
@@ -83,10 +89,12 @@ def tile_moe_res_glu_gelu_kernel(tc, x_words, x_scales, xr, w1, w3, w2, gate, of
                 nc.tensor.transpose(spread[:, e - e0, :], gate_cols[:, e : e + 1].to_broadcast([P, P]), identity[:])
             nc.scalar.copy(gate_sb[:, e0:e1, :], spread[:, : e1 - e0, :])
 
+        def list_piece(lo, hi):
+            return offsets[:, lo // SLOTS_PER_COL : hi // SLOTS_PER_COL]
+
         for lo, hi in zip(GATHER_CUTS, GATHER_CUTS[1:]):
-            piece = offsets[:, lo // PER_COL : hi // PER_COL]
-            nc.vector.tensor_copy(slot_words[:, lo:hi], tok_words[:].indirect(piece))
-            nc.vector.tensor_copy(slot_scales[:, lo:hi], tok_scales[:].indirect(piece))
+            nc.vector.tensor_copy(slot_words[:, lo:hi], tok_words[:].indirect(list_piece(lo, hi)))
+            nc.vector.tensor_copy(slot_scales[:, lo:hi], tok_scales[:].indirect(list_piece(lo, hi)))
 
         def quantize(grouped, tag):
             width = grouped.shape[1] // PACK
@@ -95,14 +103,13 @@ def tile_moe_res_glu_gelu_kernel(tc, x_words, x_scales, xr, w1, w3, w2, gate, of
             nc.vector.quantize_mx(out=codes[:].bitcast(FP8X4), scales=scales[:], in_=grouped[:])
             return codes, scales
 
-        def regroup(copy, name, e, half):
+        def half_views(name, e, half):
             grouped = ring.tile([P, PAIR * P * PACK], BF16, name=f"{name}_grouped{half}", align_bytes=64)
             dst = grouped[:].rearrange("p (t m j) -> p m j t", t=PAIR, j=PACK)
             src = raw[name, e][:].rearrange("p j (m u t) -> p u m j t", u=PACK // PAIR, t=PAIR)[:, half]
-            copy(dst, src)
-            return grouped
+            return grouped, dst, src
 
-        def multiply(sums, grouped, name, e, half):
+        def first_product(sums, grouped, name, e, half):
             codes, scales = quantize(grouped, f"{name}_{half}")
             slots = slice(e * C, (e + 1) * C)
             for t in range(PAIR):
@@ -119,9 +126,9 @@ def tile_moe_res_glu_gelu_kernel(tc, x_words, x_scales, xr, w1, w3, w2, gate, of
 
         def regroup_w2(e):
             grouped = ring.tile([P, PACK * N], BF16, name="w2_grouped", align_bytes=64)
-            dst = grouped[:].rearrange("p (c i j) -> p c j i", i=4, j=PACK)
-            src = raw["w2", e][:].rearrange("p j (c i) -> p c j i", i=4)
-            copy = nc.scalar.copy if e >= W2_ON_SCALAR_FROM else nc.vector.tensor_copy
+            dst = grouped[:].rearrange("p (c i j) -> p c j i", i=RUN, j=PACK)
+            src = raw["w2", e][:].rearrange("p j (c i) -> p c j i", i=RUN)
+            copy = nc.scalar.copy if e >= LATE_W2 else nc.vector.tensor_copy
             copy(dst, src)
             return grouped
 
@@ -142,50 +149,52 @@ def tile_moe_res_glu_gelu_kernel(tc, x_words, x_scales, xr, w1, w3, w2, gate, of
             nc.vector.tensor_tensor(gated, y[:], gate_sb[:, e, :], MULT)
 
         def scatter_results(e, gated):
-            piece = offsets[:, e * C // PER_COL : (e + 1) * C // PER_COL]
-            nc.vector.tensor_tensor(window[:].indirect(piece), gated, zeros[:], ADD)
+            nc.vector.tensor_tensor(window[:].indirect(list_piece(e * C, (e + 1) * C)), gated, zeros[:], ADD)
 
         y = h_operand = None
         for e in range(E):
             last = e == E - 1
             a = psum.tile([P, PACK, C], F32, name="a")
             b = psum.tile([P, PACK, C], F32, name="b")
-            w1_halves = [regroup(nc.scalar.copy, "w1", e, half) for half in range(2)]
-            w3_low = regroup(nc.scalar.copy, "w3", e, 0)
-            for half in range(2):
-                multiply(a, w1_halves[half], "w1", e, half)
-            w3_high = regroup(nc.vector.tensor_copy, "w3", e, 1)
+            w1_halves = []
+            for half in range(PACK // PAIR):
+                grouped, dst, src = half_views("w1", e, half)
+                nc.scalar.copy(dst, src)
+                w1_halves.append(grouped)
+            w3_low, low_dst, low_src = half_views("w3", e, 0)
+            nc.scalar.copy(low_dst[:, :SCALAR_PLACES], low_src[:, :SCALAR_PLACES])
+            for half, grouped in enumerate(w1_halves):
+                first_product(a, grouped, "w1", e, half)
+            w3_high, high_dst, high_src = half_views("w3", e, 1)
+            nc.vector.tensor_copy(high_dst, high_src)
+            nc.vector.tensor_copy(low_dst[:, SCALAR_PLACES:], low_src[:, SCALAR_PLACES:])
             if last:
                 w2_grouped = regroup_w2(e - 1)
             act = ring.tile([P, C * PACK], F32, name="act")
-            nc.scalar.activation(act[:].rearrange("p (c t) -> p c t", t=PACK), a[:].rearrange("p t c -> p c t"), GELU)
-            multiply(b, w3_high, "w3", e, 1)
-            if 0 < e < E - 1:
+            act_words = act[:].rearrange("p (c t) -> p c t", t=PACK)
+            nc.scalar.activation(act_words, a[:].rearrange("p t c -> p c t"), GELU)
+            first_product(b, w3_high, "w3", e, 1)
+            if e > 0 and not last:
                 gated = w3_high[:, : 2 * C].bitcast(F32)
                 gate_results(e - 1, y, gated)
-            multiply(b, w3_low, "w3", e, 0)
+            first_product(b, w3_low, "w3", e, 0)
             if last:
                 y = second_product(quantize(w2_grouped, "w2"), h_operand)
-            if e != E - 2:
+            if e != LATE_W2:
                 w2_grouped = regroup_w2(e)
-            if 0 < e < E - 1:
+            if e > 0 and not last:
                 scatter_results(e - 1, gated)
             h = ring.tile([P, C * PACK], BF16, name="h", align_bytes=64)
-            nc.vector.tensor_tensor(
-                h[:].rearrange("p (c t) -> p c t", t=PACK),
-                b[:].rearrange("p t c -> p c t"),
-                act[:].rearrange("p (c t) -> p c t", t=PACK),
-                MULT,
-            )
+            nc.vector.tensor_tensor(h[:].rearrange("p (c t) -> p c t", t=PACK), b[:].rearrange("p t c -> p c t"), act_words, MULT)
             if last:
                 gated = act[:, :C]
                 gate_results(e - 1, y, gated)
-            if e != E - 2:
+            if e != LATE_W2:
                 w2_operand = quantize(w2_grouped, "w2")
             h_operand = quantize(h, "h")
             if last:
                 scatter_results(e - 1, gated)
-            if e != E - 2:
+            if e != LATE_W2:
                 y = second_product(w2_operand, h_operand)
         last_gated = keep.tile([P, C], F32, name="last_gated")
         gate_results(E - 1, y, last_gated[:])

from contextlib import ExitStack

import concourse.mybir as mybir
from concourse.masks import make_identity

K, T, E, C, H, N = 512, 1280, 6, 128, 512, 128
S = E * C
FLOPS = 2 * S * (2 * K * H + H * N)

F32 = mybir.dt.float32
BF16 = mybir.dt.bfloat16
I32 = mybir.dt.int32
U32 = mybir.dt.uint32
U16 = mybir.dt.uint16
U8 = mybir.dt.uint8
FP8X4 = mybir.dt.float8_e4m3fn_x4
MULT = mybir.AluOpType.mult
ADD = mybir.AluOpType.add
GELU = mybir.ActivationFunctionType.Gelu_apprx_tanh

P = 128
PACK = 4
PAIR = 2
RUN = 4
QUADRANT = 32
SCALE_ROWS = K // 32
SLOTS_PER_COL = 16
RING = 2
GATHER_CUTS = (0, 2 * C, S)
STORE_CUTS = (0, 256, 640, 1024, T)
LATE_W2 = E - 2
SCALAR_PLACES = 88


def tile_moe_res_glu_gelu_kernel(tc, x_words, x_scales, xr, w1, w3, w2, gate, offs, out):
    nc = tc.nc
    with ExitStack() as ctx:
        keep = ctx.enter_context(tc.tile_pool(name="keep", bufs=1))
        ring = ctx.enter_context(tc.tile_pool(name="ring", bufs=RING))
        psum = ctx.enter_context(tc.psum_pool(name="psum", bufs=RING))

        offsets = keep.tile([P, S // SLOTS_PER_COL], U16, name="offsets")
        tok_words = keep.tile([P, T], U32, name="tok_words")
        tok_scales = keep.tile([P, T], U8, name="tok_scales")
        slot_words = keep.tile([P, S], U32, name="slot_words", align_bytes=64)
        slot_scales = keep.tile([P, S], U8, name="slot_scales", align_bytes=64)
        window = keep.tile([P, T], F32, name="window")
        gate_rows = keep.tile([P, C], F32, name="gate_rows")
        gate_cols = keep.tile([P, E], F32, name="gate_cols")
        gate_sb = keep.tile([P, E, C], F32, name="gate_sb")
        xr_sb = keep.tile([P, T], F32, name="xr_sb")
        zeros = keep.tile([P, C], F32, name="zeros")
        identity = keep.tile([P, P], F32, name="identity")

        nc.vector.memset(tok_scales[:].bitcast(I32), 0)
        nc.vector.memset(zeros[:], 0.0)
        make_identity(nc, identity[:])

        nc.sync.dma_start(offsets[:], offs)
        nc.sync.dma_start(tok_words[:].bitcast(I32), x_words[0].rearrange("p t r -> p (t r)").bitcast(I32))
        scale_rows = x_scales[0].bitcast(I32)
        rows_per_quadrant = SCALE_ROWS * QUADRANT // P
        for r in range(rows_per_quadrant):
            nc.scalar.dma_start(tok_scales[r:P:QUADRANT, :].bitcast(I32), scale_rows[r:SCALE_ROWS:rows_per_quadrant, :])
        nc.scalar.activation(window[:], zeros[:, 0:1].to_broadcast([P, T]), GELU)
        nc.sync.dma_start(gate_rows[:], gate.rearrange("n (e c) -> (n e) c", c=C)[0:P, :])

        raw = {}

        def load(name, w, e):
            raw[name, e] = keep.tile([P, PACK, w.shape[2]], F32, name=f"{name}_raw{e}")
            nc.sync.dma_start(raw[name, e][:], w[e].rearrange("(p j) c -> p j c", j=PACK))

        for e in range(E):
            load("w1", w1, e)
            load("w3", w3, e)
            if e < LATE_W2:
                load("w2", w2, e)
        for e in range(LATE_W2, E):
            load("w2", w2, e)
        nc.sync.dma_start(xr_sb[:], xr)

        turned = psum.tile([P, C], F32, name="y")
        nc.tensor.transpose(turned[:], gate_rows[:], identity[:])
        nc.scalar.copy(gate_cols[:], turned[:, :E])
        for tag, e0, e1 in (("a", 0, PACK), ("b", PACK, E)):
            spread = psum.tile([P, PACK, C], F32, name=tag)
            for e in range(e0, e1):
                nc.tensor.transpose(spread[:, e - e0, :], gate_cols[:, e : e + 1].to_broadcast([P, P]), identity[:])
            nc.scalar.copy(gate_sb[:, e0:e1, :], spread[:, : e1 - e0, :])

        def list_piece(lo, hi):
            return offsets[:, lo // SLOTS_PER_COL : hi // SLOTS_PER_COL]

        for lo, hi in zip(GATHER_CUTS, GATHER_CUTS[1:]):
            nc.vector.tensor_copy(slot_words[:, lo:hi], tok_words[:].indirect(list_piece(lo, hi)))
            nc.vector.tensor_copy(slot_scales[:, lo:hi], tok_scales[:].indirect(list_piece(lo, hi)))

        def quantize(grouped, tag):
            width = grouped.shape[1] // PACK
            codes = ring.tile([P, width], U32, name=tag + "_codes", align_bytes=64)
            scales = ring.tile([P, width], U8, name=tag + "_scales", align_bytes=64)
            nc.vector.quantize_mx(out=codes[:].bitcast(FP8X4), scales=scales[:], in_=grouped[:])
            return codes, scales

        def half_views(name, e, half):
            grouped = ring.tile([P, PAIR * P * PACK], BF16, name=f"{name}_grouped{half}", align_bytes=64)
            dst = grouped[:].rearrange("p (t m j) -> p m j t", t=PAIR, j=PACK)
            src = raw[name, e][:].rearrange("p j (m u t) -> p u m j t", u=PACK // PAIR, t=PAIR)[:, half]
            return grouped, dst, src

        def first_product(sums, grouped, name, e, half):
            codes, scales = quantize(grouped, f"{name}_{half}")
            slots = slice(e * C, (e + 1) * C)
            for t in range(PAIR):
                cols = slice(t * P, (t + 1) * P)
                nc.tensor.matmul_mx(
                    out=sums[:, half * PAIR + t, :],
                    lhsT=codes[:, cols].bitcast(FP8X4),
                    lhsT_scale=scales[:, cols],
                    rhs=slot_words[:, slots].bitcast(FP8X4),
                    rhs_scale=slot_scales[:, slots],
                    start=True,
                    stop=True,
                )

        def regroup_w2(e):
            grouped = ring.tile([P, PACK * N], BF16, name="w2_grouped", align_bytes=64)
            dst = grouped[:].rearrange("p (c i j) -> p c j i", i=RUN, j=PACK)
            src = raw["w2", e][:].rearrange("p j (c i) -> p c j i", i=RUN)
            copy = nc.scalar.copy if e >= LATE_W2 else nc.vector.tensor_copy
            copy(dst, src)
            return grouped

        def second_product(w_operand, h_operand):
            y = psum.tile([P, C], F32, name="y")
            nc.tensor.matmul_mx(
                out=y[:],
                lhsT=w_operand[0][:].bitcast(FP8X4),
                lhsT_scale=w_operand[1][:],
                rhs=h_operand[0][:].bitcast(FP8X4),
                rhs_scale=h_operand[1][:],
                start=True,
                stop=True,
            )
            return y

        def gate_results(e, y, gated):
            nc.vector.tensor_tensor(gated, y[:], gate_sb[:, e, :], MULT)

        def scatter_results(e, gated):
            nc.vector.tensor_tensor(window[:].indirect(list_piece(e * C, (e + 1) * C)), gated, zeros[:], ADD)

        y = h_operand = None
        for e in range(E):
            last = e == E - 1
            a = psum.tile([P, PACK, C], F32, name="a")
            b = psum.tile([P, PACK, C], F32, name="b")
            w1_halves = []
            for half in range(PACK // PAIR):
                grouped, dst, src = half_views("w1", e, half)
                nc.scalar.copy(dst, src)
                w1_halves.append(grouped)
            w3_low, low_dst, low_src = half_views("w3", e, 0)
            nc.scalar.copy(low_dst[:, :SCALAR_PLACES], low_src[:, :SCALAR_PLACES])
            for half, grouped in enumerate(w1_halves):
                first_product(a, grouped, "w1", e, half)
            w3_high, high_dst, high_src = half_views("w3", e, 1)
            nc.vector.tensor_copy(high_dst, high_src)
            nc.vector.tensor_copy(low_dst[:, SCALAR_PLACES:], low_src[:, SCALAR_PLACES:])
            if last:
                w2_grouped = regroup_w2(e - 1)
            act = ring.tile([P, C * PACK], F32, name="act")
            act_words = act[:].rearrange("p (c t) -> p c t", t=PACK)
            nc.scalar.activation(act_words, a[:].rearrange("p t c -> p c t"), GELU)
            first_product(b, w3_high, "w3", e, 1)
            if e > 0 and not last:
                gated = w3_high[:, : 2 * C].bitcast(F32)
                gate_results(e - 1, y, gated)
            first_product(b, w3_low, "w3", e, 0)
            if last:
                y = second_product(quantize(w2_grouped, "w2"), h_operand)
            if e != LATE_W2:
                w2_grouped = regroup_w2(e)
            if e > 0 and not last:
                scatter_results(e - 1, gated)
            h = ring.tile([P, C * PACK], BF16, name="h", align_bytes=64)
            nc.vector.tensor_tensor(h[:].rearrange("p (c t) -> p c t", t=PACK), b[:].rearrange("p t c -> p c t"), act_words, MULT)
            if last:
                gated = act[:, :C]
                gate_results(e - 1, y, gated)
            if e != LATE_W2:
                w2_operand = quantize(w2_grouped, "w2")
            h_operand = quantize(h, "h")
            if last:
                scatter_results(e - 1, gated)
            if e != LATE_W2:
                y = second_product(w2_operand, h_operand)
        last_gated = keep.tile([P, C], F32, name="last_gated")
        gate_results(E - 1, y, last_gated[:])
        scatter_results(E - 1, last_gated[:])

        for i, (lo, hi) in enumerate(zip(STORE_CUTS, STORE_CUTS[1:])):
            result = keep.tile([P, hi - lo], F32, name=f"result{i}")
            nc.vector.tensor_tensor(result[:], window[:, lo:hi], xr_sb[:, lo:hi], ADD)
            queue = nc.sync if i % 2 == 0 else nc.scalar
            queue.dma_start(out[:, lo:hi], result[:])
